import numpy as np
import ml_dtypes


def mxq(x, axis, fmt="e4m3"):
    dtype, down = {"e4m3": (ml_dtypes.float8_e4m3fn, 7), "e5m2": (ml_dtypes.float8_e5m2, 14)}[fmt]
    v = np.moveaxis(np.asarray(x, np.float32).astype(ml_dtypes.bfloat16).astype(np.float64), axis, -1)
    blocks = v.reshape(v.shape[:-1] + (-1, 32))
    amax = np.abs(blocks).max(-1, keepdims=True)
    byte = np.maximum(np.where(amax > 0, np.frexp(amax)[1] - 1 + 127, 0) - down, 1)
    scale = np.exp2(byte - 127.0)
    codes = (blocks / scale).astype(np.float32).astype(dtype).astype(np.float64)
    return np.moveaxis((codes * scale).reshape(v.shape), -1, axis)


WIDE = False


def mx_kscale(k):
    if not WIDE:
        return np.ones(k)
    levels = np.array([10, -10, 5, -5, 0])
    if k % 512:
        return np.exp2(np.random.permutation(np.resize(levels, k // 32))).repeat(32)
    a = np.empty((k // 512, 16))
    for p in range(k // 512):
        a[p, :8] = np.random.permutation(np.resize(levels, 8))
        for g in range(8):
            far = levels[np.abs(levels - a[p, g]) >= 10]
            a[p, g + 8] = far[np.random.randint(len(far))]
    return np.exp2(a.ravel()).repeat(32)


def f64(x):
    return np.asarray(x).astype(np.float64)


def striped(idx):
    return np.tile(idx.reshape(-1, 16).T, (8, 1)).astype(np.uint16)


def unstriped(offs):
    return offs[:16].T.reshape(-1).astype(np.int64)


E2M1 = np.array([0.0, 0.5, 1.0, 1.5, 2.0, 3.0, 4.0, 6.0, -0.0, -0.5, -1.0, -1.5, -2.0, -3.0, -4.0, -6.0])


def pack_weight(w, fmt):
    k, n = w.shape
    w = f64(np.asarray(w, np.float32).astype(ml_dtypes.bfloat16)).reshape(k // 32, 32, n)
    amax = np.abs(w).max(1)
    if fmt == "e4m3":
        byte = np.frexp(amax)[1] - 1 + 127 - 7
    else:
        mant, ex = np.frexp(amax / 6.0)
        byte = np.where(mant > 0.5, ex, ex - 1) + 127
    byte = np.clip(np.where(amax > 0, byte, 1), 1, 254)
    scaled = (w * np.exp2(127.0 - byte)[:, None, :]).reshape(k, n).astype(np.float32)
    by_word = np.ascontiguousarray(scaled.reshape(k // 512, 128, 4, n).transpose(0, 1, 3, 2))
    if fmt == "e4m3":
        words = by_word.astype(ml_dtypes.float8_e4m3fn).view(np.uint8)
    else:
        c = by_word.astype(ml_dtypes.float4_e2m1fn).view(np.uint8) & 0xF
        words = (c[..., 0::2] | (c[..., 1::2] << 4)).reshape(k // 512, 128, 2 * n)
    return np.ascontiguousarray(words), np.ascontiguousarray(byte.astype(np.uint8).reshape(k // 512, 16, n))


def unpack_weight(words, scales, fmt):
    g, _, n = scales.shape
    words = np.ascontiguousarray(words).reshape(g, 128, n, -1)
    if fmt == "e4m3":
        vals = words.view(ml_dtypes.float8_e4m3fn).astype(np.float64)
    else:
        nib = np.empty((g, 128, n, 4), np.uint8)
        nib[..., 0::2] = words & 0xF
        nib[..., 1::2] = words >> 4
        vals = E2M1[nib]
    vals = vals * np.repeat(np.exp2(scales.astype(np.float64) - 127.0), 8, axis=1)[..., None]
    return vals.transpose(0, 1, 3, 2).reshape(g * 512, n)


def relu(v):
    return np.maximum(v, 0.0)


K, T, E, C, N = 512, 768, 24, 128, 128
TOP = 4


def by_expert(wq, xq):
    return np.concatenate([wq[e].T @ xq[:, e * C:(e + 1) * C] for e in range(E)], axis=1)


def setup_inputs():
    n = np.random.standard_normal
    s = mx_kscale(K)[:, None]
    deal = np.repeat(np.arange(E), C).reshape(TOP, T)[:, np.random.permutation(T)]
    deal = np.take_along_axis(deal, np.argsort(np.random.rand(TOP, T), axis=0), axis=0)
    for _ in range(8):
        s_, t_ = np.random.permutation(T).reshape(2, -1); r = np.random.randint(TOP, size=T // 2); x, y = deal[r, s_].copy(), deal[r, t_].copy()
        ok = ~((deal[:, s_] == y).any(0) | (deal[:, t_] == x).any(0)); deal[r[ok], s_[ok]] = y[ok]; deal[r[ok], t_[ok]] = x[ok]
    order = np.lexsort((np.random.rand(TOP * T), deal.reshape(-1)))
    slot_token = order % T; pos = np.empty(TOP * T, np.int64); pos[order] = np.arange(TOP * T); pos = pos.reshape(TOP, T)
    g = np.random.uniform(0.5, 1.5, (TOP, T)); g = g / g.sum(0)
    w = [pack_weight(m, "e2m1") for m in n((E, K, N)) / np.sqrt(K) / s[None]]
    return {
        "xT": (n((K, T)) * s).astype(np.float32),
        "w_words": np.stack([m[0] for m in w]),
        "w_scales": np.stack([m[1] for m in w]),
        "b": (0.3 * n((N, E))).astype(np.float32),
        "gate": np.stack([np.tile(r, (N, 1)) for r in g]).astype(np.float32),
        "offs": striped(slot_token),
        "pos1": striped(pos[0]),
        "pos2": striped(pos[1]),
        "pos3": striped(pos[2]),
        "pos4": striped(pos[3]),
    }


def reference(xT, w_words, w_scales, b, gate, offs, pos1, pos2, pos3, pos4):
    idx = unstriped(offs)
    w = np.stack([unpack_weight(w_words[e], w_scales[e], "e2m1") for e in range(E)])
    xq = mxq(f64(xT)[:, idx], 0, "e4m3")
    y = by_expert(w, xq)
    y = relu(y + np.repeat(f64(b), C, axis=1))
    return sum(f64(gate[r]) * y[:, unstriped(p)] for r, p in enumerate((pos1, pos2, pos3, pos4)))

@@ -1,0 +1,175 @@
+from contextlib import ExitStack
+
+import concourse.mybir as mybir
+
+K, T, E, C, N, TOP = 512, 768, 24, 128, 128, 4
+P = 128
+PACK = 4
+S = E * C
+FLOPS = 2 * K * N * S
+
+F32 = mybir.dt.float32
+BF16 = mybir.dt.bfloat16
+U32 = mybir.dt.uint32
+I32 = mybir.dt.int32
+U16 = mybir.dt.uint16
+U8 = mybir.dt.uint8
+FP8X4 = mybir.dt.float8_e4m3fn_x4
+FP4X4 = mybir.dt.float4_e2m1fn_x4
+ADD, MULT, MAX = mybir.AluOpType.add, mybir.AluOpType.mult, mybir.AluOpType.max
+RELU = mybir.ActivationFunctionType.Relu
+
+X_CHUNK = 256
+SLOTS = 512
+W_LOAD = 8
+
+
+def tile_moe_tk_lin_relu_kernel(
+    tc, xT, w_words, w_scales, b, gate, offs, pos1, pos2, pos3, pos4, out
+):
+    nc = tc.nc
+    with ExitStack() as ctx:
+        keep = ctx.enter_context(tc.tile_pool(name="keep", bufs=1))
+        psum = ctx.enter_context(tc.psum_pool(name="psum", bufs=1))
+
+        x_bytes = keep.tile([P, T], U8, align_bytes=64, name="x_bytes")
+        nc.gpsimd.memset(x_bytes[:], 0)
+        w_planes = keep.tile([P, E, N], U8, align_bytes=64, name="w_planes")
+        nc.vector.memset(w_planes[:].rearrange("p e n -> p (e n)").bitcast(I32), 0)
+        warm = keep.tile([P, 8], F32, name="warm")
+        nc.vector.memset(warm[:], 0.0)
+        warm_out = keep.tile([P, 8], F32, name="warm_out")
+        nc.scalar.activation(warm_out[:], warm[:], RELU)
+
+        x_view = xT.rearrange("(p j) w -> p j w", j=PACK)
+        raws = []
+        for t0 in range(0, T, X_CHUNK):
+            raw = keep.tile([P, PACK, X_CHUNK], F32, name="raw%d" % t0)
+            nc.sync.dma_start(out=raw[:], in_=x_view[:, :, t0 : t0 + X_CHUNK])
+            raws.append(raw)
+        offs_t = keep.tile([P, S // 16], U16, name="offs_t")
+        nc.sync.dma_start(offs_t[:], offs)
+        for q in range(4):
+            nc.sync.dma_start(
+                out=w_planes[32 * q : 32 * q + 4, :, :].bitcast(I32),
+                in_=w_scales[:, 0, 4 * q : 4 * q + 4, :].rearrange("e q n -> q e n").bitcast(I32),
+            )
+        bias = keep.tile([P, E], F32, name="bias")
+        nc.sync.dma_start(out=bias[:], in_=b)
+        ws = []
+        for e0 in range(0, E, W_LOAD):
+            w = keep.tile([P, W_LOAD, 2 * N], U8, align_bytes=64, name="w%d" % e0)
+            nc.sync.dma_start(
+                out=w[:].bitcast(I32),
+                in_=w_words[e0 : e0 + W_LOAD, 0, :, :].rearrange("e p c -> p e c").bitcast(I32),
+            )
+            ws.append(w)
+        pos_ts, gates = [], []
+        for r, pos in enumerate((pos1, pos2, pos3, pos4)):
+            pos_t = keep.tile([P, T // 16], U16, name="pos_t%d" % r)
+            nc.sync.dma_start(pos_t[:], pos)
+            pos_ts.append(pos_t)
+        for r in range(TOP):
+            g = keep.tile([P, T], F32, name="gate%d" % r)
+            nc.sync.dma_start(out=g[:], in_=gate[r])
+            gates.append(g)
+
+        x_words = keep.tile([P, T], U32, align_bytes=64, name="x_words")
+
+        def interleave(i, lo, hi, copy):
+            grouped = keep.tile([P, hi - lo, PACK], BF16, align_bytes=64, name="grouped%d_%d" % (i, lo))
+            copy(out=grouped[:], in_=raws[i][:, :, lo:hi].rearrange("p j w -> p w j"))
+            return grouped
+
+        def quantise(grouped, t0, width):
+            nc.vector.quantize_mx(
+                out=x_words[:, t0 : t0 + width].bitcast(FP8X4),
+                scales=x_bytes[:, t0 : t0 + width],
+                in_=grouped[:].rearrange("p w j -> p (w j)"),
+            )
+
+        g0 = interleave(0, 0, 256, nc.vector.tensor_copy)
+        quantise(g0, 0, 256)
+        g1 = interleave(1, 0, 256, nc.vector.tensor_copy)
+        quantise(g1, 256, 256)
+        g2b = interleave(2, 128, 256, nc.scalar.copy)
+        g2a = interleave(2, 0, 128, nc.vector.tensor_copy)
+        quantise(g2a, 512, 128)
+        quantise(g2b, 640, 128)
+
+        y = keep.tile([P, S], F32, name="y")
+
+        def expert(e, words, planes, col, acc, acc_col):
+            w = ws[e // W_LOAD]
+            nc.tensor.matmul_mx(
+                out=acc[:, acc_col : acc_col + C],
+                lhsT=w[:, e % W_LOAD, :].bitcast(FP4X4),
+                lhsT_scale=w_planes[:, e, :],
+                rhs=words[:, col : col + C].bitcast(FP8X4),
+                rhs_scale=planes[:, col : col + C],
+                start=True,
+                stop=True,
+            )
+
+        def relu_scalar(e, acc, acc_col):
+            nc.scalar.activation(
+                y[:, e * C : (e + 1) * C], acc[:, acc_col : acc_col + C], RELU, bias=bias[:, e : e + 1]
+            )
+
+        def relu_vector(e, acc, acc_col):
+            nc.vector.tensor_scalar(
+                y[:, e * C : (e + 1) * C], acc[:, acc_col : acc_col + C], bias[:, e : e + 1], 0.0, op0=ADD, op1=MAX
+            )
+
+        for c in range(S // SLOTS):
+            last = c == S // SLOTS - 1
+            words = keep.tile([P, SLOTS], U32, align_bytes=64, name="words%d" % c)
+            nc.vector.tensor_copy(words[:], x_words[:].indirect(offs_t[:, 32 * c : 32 * (c + 1)]))
+            half = SLOTS // 2 if last else SLOTS
+            e0 = c * SLOTS // C
+            for h in range(SLOTS // half):
+                planes = keep.tile([P, half], U8, align_bytes=64, name="planes%d_%d" % (c, h))
+                o = (c * SLOTS + h * half) // 16
+                nc.vector.tensor_copy(planes[:], x_bytes[:].indirect(offs_t[:, o : o + half // 16]))
+                n = half // C
+                if not last or h == 0:
+                    acc = psum.tile([P, 512], F32, name="acc%d_%d" % (c, h))
+                    for i in range(n):
+                        expert(e0 + h * n + i, words[:, h * half :], planes, i * C, acc, i * C)
+                    for i in range(n):
+                        relu_scalar(e0 + h * n + i, acc, i * C)
+                else:
+                    accs = []
+                    for i in range(n):
+                        acc = psum.tile([P, 512], F32, name="acc%d_%d_%d" % (c, h, i))
+                        expert(e0 + h * n + i, words[:, h * half :], planes, i * C, acc, 0)
+                        accs.append(acc)
+                    relu_scalar(E - 2, accs[0], 0)
+                    relu_vector(E - 1, accs[1], 0)
+
+        prods = []
+        for r in range(TOP):
+            prod = keep.tile([P, T], F32, name="prod%d" % r)
+            prods.append(prod)
+
+        def fetch(r, lo, hi):
+            nc.vector.tensor_tensor(
+                prods[r][:, lo:hi], y[:].indirect(pos_ts[r][:, lo // 16 : hi // 16]), gates[r][:, lo:hi], MULT
+            )
+
+        cut = 512
+        s01 = keep.tile([P, T], F32, name="s01")
+        s012 = keep.tile([P, T], F32, name="s012")
+        res_a = keep.tile([P, cut], F32, name="res_a")
+        res_b = keep.tile([P, T - cut], F32, name="res_b")
+        fetch(0, 0, T)
+        fetch(1, 0, T)
+        fetch(2, 0, T)
+        nc.vector.tensor_tensor(s01[:], prods[0][:], prods[1][:], ADD)
+        fetch(3, 0, cut)
+        nc.vector.tensor_tensor(s012[:], s01[:], prods[2][:], ADD)
+        fetch(3, cut, T)
+        nc.vector.tensor_tensor(res_a[:], s012[:, 0:cut], prods[3][:, 0:cut], ADD)
+        nc.sync.dma_start(out=out[:, 0:cut], in_=res_a[:])
+        nc.vector.tensor_tensor(res_b[:], s012[:, cut:T], prods[3][:, cut:T], ADD)
+        nc.sync.dma_start(out=out[:, cut:T], in_=res_b[:])

@@ -1,6 +1,7 @@
 from contextlib import ExitStack
 
 import concourse.mybir as mybir
+from concourse.masks import make_identity
 
 K, T, E, C, N, TOP = 512, 768, 24, 128, 128, 4
 P = 128
@@ -19,8 +20,9 @@ FP4X4 = mybir.dt.float4_e2m1fn_x4
 ADD, MULT, MAX = mybir.AluOpType.add, mybir.AluOpType.mult, mybir.AluOpType.max
 RELU = mybir.ActivationFunctionType.Relu
 
-X_CHUNK = 256
-SLOTS = 512
+X_CUTS = (0, 256, 512, 640, 768)
+WINDOW = 2048
+GROUP = 8
 W_LOAD = 8
 
 
@@ -32,8 +34,8 @@ def tile_moe_tk_lin_relu_kernel(
         keep = ctx.enter_context(tc.tile_pool(name="keep", bufs=1))
         psum = ctx.enter_context(tc.psum_pool(name="psum", bufs=1))
 
-        x_bytes = keep.tile([P, T], U8, align_bytes=64, name="x_bytes")
-        nc.gpsimd.memset(x_bytes[:], 0)
+        x_bytes = keep.tile([P, WINDOW], U8, align_bytes=64, name="x_bytes")
+        nc.gpsimd.memset(x_bytes[:, 0:T], 0)
         w_planes = keep.tile([P, E, N], U8, align_bytes=64, name="w_planes")
         nc.vector.memset(w_planes[:].rearrange("p e n -> p (e n)").bitcast(I32), 0)
         warm = keep.tile([P, 8], F32, name="warm")
@@ -41,11 +43,14 @@ def tile_moe_tk_lin_relu_kernel(
         warm_out = keep.tile([P, 8], F32, name="warm_out")
         nc.scalar.activation(warm_out[:], warm[:], RELU)
 
+        ident = keep.tile([P, P], F32, name="ident")
+        make_identity(nc, ident[:])
+
         x_view = xT.rearrange("(p j) w -> p j w", j=PACK)
         raws = []
-        for t0 in range(0, T, X_CHUNK):
-            raw = keep.tile([P, PACK, X_CHUNK], F32, name="raw%d" % t0)
-            nc.sync.dma_start(out=raw[:], in_=x_view[:, :, t0 : t0 + X_CHUNK])
+        for t0, t1 in zip(X_CUTS[:-1], X_CUTS[1:]):
+            raw = keep.tile([P, PACK, t1 - t0], F32, name="raw%d" % t0)
+            nc.sync.dma_start(out=raw[:], in_=x_view[:, :, t0:t1])
             raws.append(raw)
         offs_t = keep.tile([P, S // 16], U16, name="offs_t")
         nc.sync.dma_start(offs_t[:], offs)
@@ -74,28 +79,24 @@ def tile_moe_tk_lin_relu_kernel(
             nc.sync.dma_start(out=g[:], in_=gate[r])
             gates.append(g)
 
-        x_words = keep.tile([P, T], U32, align_bytes=64, name="x_words")
+        x_words = keep.tile([P, WINDOW], U32, align_bytes=64, name="x_words")
 
-        def interleave(i, lo, hi, copy):
-            grouped = keep.tile([P, hi - lo, PACK], BF16, align_bytes=64, name="grouped%d_%d" % (i, lo))
-            copy(out=grouped[:], in_=raws[i][:, :, lo:hi].rearrange("p j w -> p w j"))
-            return grouped
+        def interleave(i, grouped, o):
+            width = X_CUTS[i + 1] - X_CUTS[i]
+            share = width * 5 // 8
+            source = raws[i][:].rearrange("p j w -> p w j")
+            nc.scalar.copy(out=grouped[:, o + share : o + width, :], in_=source[:, share:width, :])
+            nc.vector.tensor_copy(out=grouped[:, o : o + share, :], in_=source[:, 0:share, :])
 
-        def quantise(grouped, t0, width):
+        for q, parts in enumerate(((0,), (1,), (2, 3))):
+            grouped = keep.tile([P, 256, PACK], BF16, align_bytes=64, name="grouped%d" % q)
+            for i in parts:
+                interleave(i, grouped, X_CUTS[i] - 256 * q)
             nc.vector.quantize_mx(
-                out=x_words[:, t0 : t0 + width].bitcast(FP8X4),
-                scales=x_bytes[:, t0 : t0 + width],
+                out=x_words[:, 256 * q : 256 * (q + 1)].bitcast(FP8X4),
+                scales=x_bytes[:, 256 * q : 256 * (q + 1)],
                 in_=grouped[:].rearrange("p w j -> p (w j)"),
             )
-
-        g0 = interleave(0, 0, 256, nc.vector.tensor_copy)
-        quantise(g0, 0, 256)
-        g1 = interleave(1, 0, 256, nc.vector.tensor_copy)
-        quantise(g1, 256, 256)
-        g2b = interleave(2, 128, 256, nc.scalar.copy)
-        g2a = interleave(2, 0, 128, nc.vector.tensor_copy)
-        quantise(g2a, 512, 128)
-        quantise(g2b, 640, 128)
 
         y = keep.tile([P, S], F32, name="y")
 
@@ -121,31 +122,40 @@ def tile_moe_tk_lin_relu_kernel(
                 y[:, e * C : (e + 1) * C], acc[:, acc_col : acc_col + C], bias[:, e : e + 1], 0.0, op0=ADD, op1=MAX
             )
 
-        for c in range(S // SLOTS):
-            last = c == S // SLOTS - 1
-            words = keep.tile([P, SLOTS], U32, align_bytes=64, name="words%d" % c)
-            nc.vector.tensor_copy(words[:], x_words[:].indirect(offs_t[:, 32 * c : 32 * (c + 1)]))
-            half = SLOTS // 2 if last else SLOTS
-            e0 = c * SLOTS // C
-            for h in range(SLOTS // half):
-                planes = keep.tile([P, half], U8, align_bytes=64, name="planes%d_%d" % (c, h))
-                o = (c * SLOTS + h * half) // 16
-                nc.vector.tensor_copy(planes[:], x_bytes[:].indirect(offs_t[:, o : o + half // 16]))
-                n = half // C
-                if not last or h == 0:
-                    acc = psum.tile([P, 512], F32, name="acc%d_%d" % (c, h))
-                    for i in range(n):
-                        expert(e0 + h * n + i, words[:, h * half :], planes, i * C, acc, i * C)
-                    for i in range(n):
-                        relu_scalar(e0 + h * n + i, acc, i * C)
-                else:
-                    accs = []
-                    for i in range(n):
-                        acc = psum.tile([P, 512], F32, name="acc%d_%d_%d" % (c, h, i))
-                        expert(e0 + h * n + i, words[:, h * half :], planes, i * C, acc, 0)
-                        accs.append(acc)
-                    relu_scalar(E - 2, accs[0], 0)
-                    relu_vector(E - 1, accs[1], 0)
+        def gather_words(e0, n):
+            words = keep.tile([P, n * C], U32, align_bytes=64, name="words%d" % e0)
+            nc.vector.tensor_copy(words[:], x_words[:].indirect(offs_t[:, e0 * C // 16 : (e0 + n) * C // 16]))
+            return words
+
+        def gather_planes(e0, n):
+            planes = keep.tile([P, n * C], U8, align_bytes=64, name="planes%d" % e0)
+            window = x_bytes[:, 0:1024] if n == 1 else x_bytes[:]
+            nc.vector.tensor_copy(planes[:], window.indirect(offs_t[:, e0 * C // 16 : (e0 + n) * C // 16]))
+            return planes
+
+        banks_used = []
+
+        def experts(e0, n, words, planes):
+            acc = psum.tile([P, 512], F32, name="bank%d" % (len(banks_used) % 8))
+            banks_used.append(e0)
+            for i in range(n):
+                expert(e0 + i, words[:, i * C :], planes[:, i * C :], 0, acc, i * C)
+            return acc
+
+        for e0 in range(0, E, GROUP):
+            words = gather_words(e0, GROUP)
+            first = e0
+            for n in (8,) if e0 + GROUP < E else (4, 2, 1, 1):
+                planes = gather_planes(first, n)
+                m = min(4, n)
+                for h in range(0, n, m):
+                    acc = experts(first + h, m, words[:, (first + h - e0) * C :], planes[:, h * C :])
+                    for i in range(m):
+                        if first + h + i < E - 2:
+                            relu_scalar(first + h + i, acc, i * C)
+                        else:
+                            relu_vector(first + h + i, acc, i * C)
+                first += n
 
         prods = []
         for r in range(TOP):
@@ -157,19 +167,42 @@ def tile_moe_tk_lin_relu_kernel(
                 prods[r][:, lo:hi], y[:].indirect(pos_ts[r][:, lo // 16 : hi // 16]), gates[r][:, lo:hi], MULT
             )
 
-        cut = 512
-        s01 = keep.tile([P, T], F32, name="s01")
-        s012 = keep.tile([P, T], F32, name="s012")
-        res_a = keep.tile([P, cut], F32, name="res_a")
-        res_b = keep.tile([P, T - cut], F32, name="res_b")
-        fetch(0, 0, T)
-        fetch(1, 0, T)
-        fetch(2, 0, T)
-        nc.vector.tensor_tensor(s01[:], prods[0][:], prods[1][:], ADD)
-        fetch(3, 0, cut)
-        nc.vector.tensor_tensor(s012[:], s01[:], prods[2][:], ADD)
-        fetch(3, cut, T)
-        nc.vector.tensor_tensor(res_a[:], s012[:, 0:cut], prods[3][:, 0:cut], ADD)
-        nc.sync.dma_start(out=out[:, 0:cut], in_=res_a[:])
-        nc.vector.tensor_tensor(res_b[:], s012[:, cut:T], prods[3][:, cut:T], ADD)
-        nc.sync.dma_start(out=out[:, cut:T], in_=res_b[:])
+        blocks = T // P
+        sums_t = []
+        for k in range(blocks):
+            sum_t = psum.tile([P, 512], F32, name="bank%d" % k)
+            sums_t.append(sum_t)
+        back_a = psum.tile([P, 512], F32, name="bank6")
+        back_b = psum.tile([P, 512], F32, name="bank7")
+
+        def add_turned(r, k):
+            nc.tensor.matmul(
+                out=sums_t[k][:, 0:P],
+                lhsT=prods[r][:, k * P : (k + 1) * P],
+                rhs=ident[:],
+                is_transpose=True,
+                start=r == 0,
+                stop=r == TOP - 2,
+            )
+
+        def turn_back(k):
+            turned = keep.tile([P, P], F32, name="turned%d" % k)
+            nc.scalar.copy(turned[:], sums_t[k][:, 0:P])
+            nc.tensor.transpose((back_a if k < 3 else back_b)[:, k % 3 * P : (k % 3 + 1) * P], turned[:], ident[:])
+
+        for r in range(TOP - 2):
+            fetch(r, 0, T)
+            for k in range(blocks):
+                add_turned(r, k)
+        for h in range(2):
+            fetch(TOP - 2, h * 384, (h + 1) * 384)
+            for k in range(3 * h, 3 * h + 3):
+                add_turned(TOP - 2, k)
+            for k in range(3 * h, 3 * h + 3):
+                turn_back(k)
+        fetch(3, 0, T)
+        for t0, t1, back in ((0, 384, back_a), (384, 640, back_b), (640, 768, back_b)):
+            res = keep.tile([P, t1 - t0], F32, name="res%d" % t0)
+            o = t0 % 384
+            nc.vector.tensor_tensor(res[:], back[:, o : o + t1 - t0], prods[3][:, t0:t1], ADD)
+            nc.sync.dma_start(out=out[:, t0:t1], in_=res[:])

from contextlib import ExitStack

import concourse.mybir as mybir
from concourse.masks import make_identity

K, T, E, C, N, TOP = 512, 768, 24, 128, 128, 4
P = 128
PACK = 4
S = E * C
FLOPS = 2 * K * N * S

F32 = mybir.dt.float32
BF16 = mybir.dt.bfloat16
U32 = mybir.dt.uint32
I32 = mybir.dt.int32
U16 = mybir.dt.uint16
U8 = mybir.dt.uint8
FP8X4 = mybir.dt.float8_e4m3fn_x4
FP4X4 = mybir.dt.float4_e2m1fn_x4
ADD, MULT, MAX = mybir.AluOpType.add, mybir.AluOpType.mult, mybir.AluOpType.max
RELU = mybir.ActivationFunctionType.Relu

X_CUTS = (0, 256, 512, 640, 768)
WINDOW = 2048
GROUP = 8
W_LOAD = 8


def tile_moe_tk_lin_relu_kernel(
    tc, xT, w_words, w_scales, b, gate, offs, pos1, pos2, pos3, pos4, out
):
    nc = tc.nc
    with ExitStack() as ctx:
        keep = ctx.enter_context(tc.tile_pool(name="keep", bufs=1))
        psum = ctx.enter_context(tc.psum_pool(name="psum", bufs=1))

        x_bytes = keep.tile([P, WINDOW], U8, align_bytes=64, name="x_bytes")
        nc.gpsimd.memset(x_bytes[:, 0:T], 0)
        w_planes = keep.tile([P, E, N], U8, align_bytes=64, name="w_planes")
        nc.vector.memset(w_planes[:].rearrange("p e n -> p (e n)").bitcast(I32), 0)
        warm = keep.tile([P, 8], F32, name="warm")
        nc.vector.memset(warm[:], 0.0)
        warm_out = keep.tile([P, 8], F32, name="warm_out")
        nc.scalar.activation(warm_out[:], warm[:], RELU)

        ident = keep.tile([P, P], F32, name="ident")
        make_identity(nc, ident[:])

        x_view = xT.rearrange("(p j) w -> p j w", j=PACK)
        raws = []
        for t0, t1 in zip(X_CUTS[:-1], X_CUTS[1:]):
            raw = keep.tile([P, PACK, t1 - t0], F32, name="raw%d" % t0)
            nc.sync.dma_start(out=raw[:], in_=x_view[:, :, t0:t1])
            raws.append(raw)
        offs_t = keep.tile([P, S // 16], U16, name="offs_t")
        nc.sync.dma_start(offs_t[:], offs)
        for q in range(4):
            nc.sync.dma_start(
                out=w_planes[32 * q : 32 * q + 4, :, :].bitcast(I32),
                in_=w_scales[:, 0, 4 * q : 4 * q + 4, :].rearrange("e q n -> q e n").bitcast(I32),
            )
        bias = keep.tile([P, E], F32, name="bias")
        nc.sync.dma_start(out=bias[:], in_=b)
        ws = []
        for e0 in range(0, E, W_LOAD):
            w = keep.tile([P, W_LOAD, 2 * N], U8, align_bytes=64, name="w%d" % e0)
            nc.sync.dma_start(
                out=w[:].bitcast(I32),
                in_=w_words[e0 : e0 + W_LOAD, 0, :, :].rearrange("e p c -> p e c").bitcast(I32),
            )
            ws.append(w)
        pos_ts, gates = [], []
        for r, pos in enumerate((pos1, pos2, pos3, pos4)):
            pos_t = keep.tile([P, T // 16], U16, name="pos_t%d" % r)
            nc.sync.dma_start(pos_t[:], pos)
            pos_ts.append(pos_t)
        for r in range(TOP):
            g = keep.tile([P, T], F32, name="gate%d" % r)
            nc.sync.dma_start(out=g[:], in_=gate[r])
            gates.append(g)

        x_words = keep.tile([P, WINDOW], U32, align_bytes=64, name="x_words")

        def interleave(i, grouped, o):
            width = X_CUTS[i + 1] - X_CUTS[i]
            share = width * 5 // 8
            source = raws[i][:].rearrange("p j w -> p w j")
            nc.scalar.copy(out=grouped[:, o + share : o + width, :], in_=source[:, share:width, :])
            nc.vector.tensor_copy(out=grouped[:, o : o + share, :], in_=source[:, 0:share, :])

        for q, parts in enumerate(((0,), (1,), (2, 3))):
            grouped = keep.tile([P, 256, PACK], BF16, align_bytes=64, name="grouped%d" % q)
            for i in parts:
                interleave(i, grouped, X_CUTS[i] - 256 * q)
            nc.vector.quantize_mx(
                out=x_words[:, 256 * q : 256 * (q + 1)].bitcast(FP8X4),
                scales=x_bytes[:, 256 * q : 256 * (q + 1)],
                in_=grouped[:].rearrange("p w j -> p (w j)"),
            )

        y = keep.tile([P, S], F32, name="y")

        def expert(e, words, planes, col, acc, acc_col):
            w = ws[e // W_LOAD]
            nc.tensor.matmul_mx(
                out=acc[:, acc_col : acc_col + C],
                lhsT=w[:, e % W_LOAD, :].bitcast(FP4X4),
                lhsT_scale=w_planes[:, e, :],
                rhs=words[:, col : col + C].bitcast(FP8X4),
                rhs_scale=planes[:, col : col + C],
                start=True,
                stop=True,
            )

        def relu_scalar(e, acc, acc_col):
            nc.scalar.activation(
                y[:, e * C : (e + 1) * C], acc[:, acc_col : acc_col + C], RELU, bias=bias[:, e : e + 1]
            )

        def relu_vector(e, acc, acc_col):
            nc.vector.tensor_scalar(
                y[:, e * C : (e + 1) * C], acc[:, acc_col : acc_col + C], bias[:, e : e + 1], 0.0, op0=ADD, op1=MAX
            )

        def gather_words(e0, n):
            words = keep.tile([P, n * C], U32, align_bytes=64, name="words%d" % e0)
            nc.vector.tensor_copy(words[:], x_words[:].indirect(offs_t[:, e0 * C // 16 : (e0 + n) * C // 16]))
            return words

        def gather_planes(e0, n):
            planes = keep.tile([P, n * C], U8, align_bytes=64, name="planes%d" % e0)
            window = x_bytes[:, 0:1024] if n == 1 else x_bytes[:]
            nc.vector.tensor_copy(planes[:], window.indirect(offs_t[:, e0 * C // 16 : (e0 + n) * C // 16]))
            return planes

        banks_used = []

        def experts(e0, n, words, planes):
            acc = psum.tile([P, 512], F32, name="bank%d" % (len(banks_used) % 8))
            banks_used.append(e0)
            for i in range(n):
                expert(e0 + i, words[:, i * C :], planes[:, i * C :], 0, acc, i * C)
            return acc

        for e0 in range(0, E, GROUP):
            words = gather_words(e0, GROUP)
            first = e0
            for n in (8,) if e0 + GROUP < E else (4, 2, 1, 1):
                planes = gather_planes(first, n)
                m = min(4, n)
                for h in range(0, n, m):
                    acc = experts(first + h, m, words[:, (first + h - e0) * C :], planes[:, h * C :])
                    for i in range(m):
                        if first + h + i < E - 2:
                            relu_scalar(first + h + i, acc, i * C)
                        else:
                            relu_vector(first + h + i, acc, i * C)
                first += n

        prods = []
        for r in range(TOP):
            prod = keep.tile([P, T], F32, name="prod%d" % r)
            prods.append(prod)

        def fetch(r, lo, hi):
            nc.vector.tensor_tensor(
                prods[r][:, lo:hi], y[:].indirect(pos_ts[r][:, lo // 16 : hi // 16]), gates[r][:, lo:hi], MULT
            )

        blocks = T // P
        sums_t = []
        for k in range(blocks):
            sum_t = psum.tile([P, 512], F32, name="bank%d" % k)
            sums_t.append(sum_t)
        back_a = psum.tile([P, 512], F32, name="bank6")
        back_b = psum.tile([P, 512], F32, name="bank7")

        def add_turned(r, k):
            nc.tensor.matmul(
                out=sums_t[k][:, 0:P],
                lhsT=prods[r][:, k * P : (k + 1) * P],
                rhs=ident[:],
                is_transpose=True,
                start=r == 0,
                stop=r == TOP - 2,
            )

        def turn_back(k):
            turned = keep.tile([P, P], F32, name="turned%d" % k)
            nc.scalar.copy(turned[:], sums_t[k][:, 0:P])
            nc.tensor.transpose((back_a if k < 3 else back_b)[:, k % 3 * P : (k % 3 + 1) * P], turned[:], ident[:])

        for r in range(TOP - 2):
            fetch(r, 0, T)
            for k in range(blocks):
                add_turned(r, k)
        for h in range(2):
            fetch(TOP - 2, h * 384, (h + 1) * 384)
            for k in range(3 * h, 3 * h + 3):
                add_turned(TOP - 2, k)
            for k in range(3 * h, 3 * h + 3):
                turn_back(k)
        fetch(3, 0, T)
        for t0, t1, back in ((0, 384, back_a), (384, 640, back_b), (640, 768, back_b)):
            res = keep.tile([P, t1 - t0], F32, name="res%d" % t0)
            o = t0 % 384
            nc.vector.tensor_tensor(res[:], back[:, o : o + t1 - t0], prods[3][:, t0:t1], ADD)
            nc.sync.dma_start(out=out[:, t0:t1], in_=res[:])
